import numpy as np, ml_dtypes
CORES = [73,201,329,457,330]
N = 5
TOK, K, FT = 512, 1, 1
ROUTE = [[[4],[2],[4],[1],[2],[0],[4],[2],[2],[1],[2],[2],[2],[4],[0],[4],[1],[1],[3],[3],[4],[3],[2],[0],[0],[2],[3],[2],[3],[2],[1],[4],[0],[3],[3],[1],[0],[3],[0],[1],[4],[1],[2],[0],[3],[1],[3],[3],[1],[2],[0],[2],[0],[2],[3],[2],[2],[3],[2],[1],[1],[4],[3],[0],[4],[0],[0],[3],[4],[4],[3],[3],[3],[0],[2],[1],[0],[3],[3],[3],[3],[2],[1],[3],[0],[3],[3],[2],[2],[4],[0],[0],[1],[1],[2],[4],[0],[2],[1],[3],[0],[1],[1],[0],[3],[0],[4],[2],[3],[4],[0],[1],[4],[4],[1],[1],[1],[2],[0],[0],[4],[1],[3],[4],[2],[2],[3],[0],[1],[2],[2],[4],[4],[3],[0],[2],[0],[3],[0],[4],[2],[1],[1],[0],[4],[3],[4],[1],[3],[2],[1],[3],[3],[4],[3],[4],[0],[3],[4],[2],[2],[4],[4],[2],[0],[4],[2],[1],[2],[0],[2],[0],[3],[3],[3],[4],[1],[0],[1],[2],[2],[2],[0],[0],[2],[2],[3],[2],[0],[1],[2],[1],[2],[3],[3],[0],[1],[3],[2],[3],[3],[3],[0],[3],[2],[4],[1],[2],[4],[4],[3],[0],[3],[0],[2],[0],[3],[2],[0],[3],[1],[3],[4],[3],[1],[3],[2],[2],[2],[0],[1],[1],[0],[0],[4],[2],[1],[3],[0],[2],[4],[4],[1],[3],[4],[4],[1],[0],[2],[0],[2],[2],[1],[4],[4],[1],[2],[0],[2],[2],[0],[0],[0],[2],[4],[3],[2],[2],[3],[0],[0],[3],[1],[3],[2],[0],[1],[3],[4],[1],[3],[3],[3],[1],[4],[0],[0],[3],[3],[3],[2],[2],[0],[1],[2],[3],[1],[3],[1],[4],[3],[4],[3],[3],[4],[2],[3],[1],[1],[0],[0],[1],[2],[2],[3],[3],[2],[1],[4],[4],[3],[1],[0],[2],[0],[0],[1],[0],[1],[1],[3],[0],[2],[2],[0],[3],[1],[2],[2],[4],[4],[0],[2],[3],[0],[3],[1],[3],[4],[0],[0],[2],[2],[4],[4],[3],[2],[4],[2],[3],[1],[0],[4],[1],[0],[1],[4],[1],[4],[1],[2],[1],[3],[2],[4],[0],[2],[3],[3],[3],[1],[4],[2],[4],[3],[1],[2],[3],[1],[3],[1],[3],[2],[4],[1],[2],[3],[4],[2],[1],[4],[3],[0],[3],[4],[3],[4],[2],[0],[4],[3],[4],[3],[2],[4],[0],[3],[2],[2],[2],[0],[0],[2],[3],[2],[3],[0],[3],[1],[3],[4],[2],[0],[2],[0],[3],[2],[4],[4],[2],[2],[2],[4],[3],[3],[4],[0],[1],[0],[0],[4],[2],[0],[1],[4],[1],[2],[3],[0],[0],[2],[0],[2],[4],[1],[2],[1],[4],[3],[0],[1],[0],[1],[3],[1],[0],[3],[1],[0],[2],[2],[0],[0],[1],[3],[1],[1],[0],[0],[4],[2],[0],[2],[4],[4],[4],[3],[2],[0],[3],[3],[4],[0],[1],[4],[1],[0],[0],[3],[0],[2],[3]],[[2],[0],[0],[1],[2],[3],[1],[3],[3],[4],[0],[3],[0],[0],[3],[4],[1],[0],[2],[3],[2],[4],[0],[3],[4],[4],[0],[3],[1],[1],[4],[0],[3],[4],[4],[1],[2],[3],[4],[0],[2],[4],[1],[2],[1],[2],[2],[3],[1],[2],[3],[4],[3],[2],[4],[3],[2],[3],[4],[1],[1],[3],[0],[1],[2],[0],[4],[3],[2],[4],[4],[3],[1],[4],[4],[4],[4],[1],[1],[4],[1],[2],[4],[1],[2],[3],[1],[4],[0],[4],[2],[3],[3],[1],[0],[0],[4],[0],[3],[0],[0],[0],[4],[0],[3],[1],[3],[4],[1],[0],[3],[1],[3],[2],[0],[2],[0],[1],[1],[3],[1],[0],[2],[2],[4],[2],[4],[1],[3],[2],[0],[0],[1],[4],[3],[1],[2],[1],[3],[0],[0],[4],[2],[0],[0],[0],[1],[1],[4],[0],[4],[1],[3],[0],[4],[4],[0],[4],[0],[3],[2],[3],[0],[2],[1],[4],[1],[2],[0],[1],[2],[0],[0],[2],[3],[2],[4],[4],[4],[2],[0],[3],[3],[2],[4],[0],[4],[3],[2],[1],[0],[0],[1],[1],[1],[0],[4],[3],[4],[2],[0],[2],[3],[3],[0],[4],[4],[2],[0],[2],[2],[2],[3],[1],[3],[1],[0],[0],[0],[1],[3],[4],[2],[3],[4],[0],[3],[1],[1],[2],[3],[3],[2],[1],[0],[0],[1],[4],[3],[1],[0],[0],[0],[1],[3],[1],[3],[1],[2],[4],[1],[2],[3],[1],[2],[2],[2],[2],[3],[4],[0],[2],[1],[3],[4],[3],[2],[0],[0],[3],[4],[0],[1],[4],[1],[4],[4],[4],[4],[4],[2],[1],[3],[2],[0],[4],[3],[1],[3],[4],[0],[3],[4],[3],[2],[3],[2],[3],[0],[0],[2],[0],[3],[0],[0],[3],[2],[4],[1],[4],[4],[1],[3],[4],[3],[0],[3],[3],[0],[0],[0],[4],[0],[0],[4],[3],[3],[1],[0],[0],[3],[4],[3],[2],[0],[0],[2],[2],[3],[3],[4],[3],[1],[3],[3],[1],[0],[3],[3],[3],[4],[0],[1],[4],[2],[3],[2],[2],[2],[3],[0],[3],[4],[0],[2],[1],[1],[3],[1],[4],[0],[4],[4],[1],[0],[1],[1],[2],[3],[1],[4],[4],[3],[2],[1],[3],[0],[2],[4],[1],[1],[0],[2],[4],[0],[1],[3],[3],[4],[3],[2],[2],[0],[3],[2],[3],[2],[3],[0],[2],[1],[2],[3],[0],[2],[0],[3],[4],[3],[2],[4],[1],[1],[2],[2],[0],[4],[3],[1],[0],[4],[2],[4],[4],[3],[4],[2],[0],[2],[3],[2],[0],[4],[4],[3],[1],[4],[4],[2],[3],[0],[4],[2],[1],[3],[2],[3],[2],[1],[2],[2],[1],[0],[0],[0],[0],[2],[3],[2],[3],[4],[0],[3],[1],[4],[1],[4],[0],[0],[1],[3],[0],[4],[3],[4],[1],[3],[3],[3],[1],[2],[2],[0],[0],[2],[2],[3],[4],[0],[0],[1],[4],[3],[4],[0],[1],[0],[2],[3],[4],[4],[0]],[[4],[3],[0],[4],[4],[3],[1],[1],[3],[0],[2],[2],[3],[1],[0],[4],[3],[4],[2],[2],[3],[1],[0],[1],[4],[4],[0],[0],[3],[3],[1],[2],[0],[1],[1],[4],[4],[1],[0],[2],[1],[1],[2],[2],[1],[4],[3],[0],[0],[3],[3],[3],[0],[3],[3],[4],[3],[3],[4],[2],[0],[2],[4],[1],[1],[2],[4],[4],[2],[3],[1],[2],[1],[0],[4],[0],[0],[3],[2],[3],[4],[0],[4],[1],[4],[4],[0],[1],[4],[4],[4],[2],[1],[2],[0],[3],[1],[3],[1],[2],[2],[3],[3],[3],[2],[0],[1],[4],[2],[1],[0],[2],[2],[2],[3],[1],[0],[4],[4],[2],[2],[2],[2],[3],[1],[0],[2],[2],[0],[3],[3],[2],[2],[1],[1],[4],[4],[4],[0],[4],[0],[4],[2],[3],[4],[2],[0],[1],[2],[0],[0],[2],[1],[1],[3],[3],[2],[3],[3],[1],[2],[0],[0],[0],[4],[1],[1],[0],[4],[0],[4],[2],[3],[4],[0],[4],[0],[0],[3],[3],[1],[0],[1],[4],[2],[4],[3],[0],[0],[0],[1],[3],[2],[1],[3],[2],[4],[3],[3],[4],[0],[0],[4],[1],[4],[2],[1],[1],[2],[3],[1],[1],[0],[3],[0],[4],[0],[1],[2],[4],[3],[4],[2],[1],[4],[2],[3],[4],[0],[4],[3],[4],[2],[4],[1],[2],[4],[0],[0],[1],[3],[0],[3],[3],[2],[1],[2],[4],[1],[2],[0],[4],[4],[1],[0],[2],[1],[2],[4],[1],[2],[0],[1],[2],[0],[4],[3],[4],[3],[2],[4],[1],[0],[3],[1],[4],[4],[3],[0],[0],[3],[3],[1],[0],[2],[2],[1],[3],[2],[1],[2],[3],[1],[4],[0],[3],[4],[4],[4],[1],[0],[4],[0],[2],[2],[2],[4],[0],[1],[0],[2],[0],[3],[3],[1],[3],[0],[4],[0],[2],[2],[4],[3],[2],[0],[3],[4],[3],[4],[3],[2],[0],[1],[1],[2],[2],[4],[4],[1],[4],[4],[2],[3],[1],[2],[1],[1],[2],[3],[0],[3],[4],[4],[0],[2],[0],[4],[0],[1],[0],[1],[1],[4],[1],[1],[3],[2],[3],[0],[3],[3],[1],[3],[4],[2],[4],[3],[0],[3],[4],[3],[2],[3],[2],[3],[3],[3],[1],[3],[2],[0],[2],[0],[4],[1],[2],[4],[3],[3],[4],[0],[1],[3],[1],[0],[2],[4],[1],[0],[1],[4],[0],[2],[0],[2],[0],[1],[4],[4],[2],[3],[3],[2],[3],[0],[1],[1],[3],[1],[1],[1],[1],[1],[1],[2],[2],[0],[0],[4],[0],[0],[4],[4],[2],[2],[2],[1],[0],[1],[0],[3],[0],[2],[0],[0],[0],[4],[2],[4],[2],[3],[0],[0],[2],[1],[1],[2],[1],[1],[1],[2],[4],[2],[2],[2],[0],[3],[0],[1],[2],[0],[4],[0],[2],[3],[2],[1],[3],[1],[2],[2],[2],[2],[4],[1],[2],[1],[2],[3],[1],[3],[4],[2],[2],[2],[3],[1],[4],[0],[1],[2],[4]],[[2],[4],[4],[2],[0],[2],[2],[1],[1],[3],[0],[0],[0],[3],[2],[0],[3],[3],[4],[4],[1],[2],[0],[2],[2],[1],[4],[2],[2],[0],[4],[3],[1],[2],[1],[0],[0],[0],[4],[4],[2],[4],[1],[0],[3],[2],[3],[2],[3],[3],[0],[3],[4],[3],[0],[2],[2],[1],[4],[2],[2],[4],[3],[1],[1],[4],[3],[2],[3],[0],[4],[4],[3],[0],[1],[4],[2],[3],[4],[4],[1],[2],[3],[4],[1],[3],[0],[1],[3],[4],[2],[1],[3],[4],[3],[1],[2],[0],[4],[0],[1],[2],[4],[2],[4],[1],[0],[3],[1],[4],[4],[1],[0],[2],[2],[1],[1],[4],[2],[3],[3],[0],[0],[0],[4],[4],[1],[1],[4],[3],[4],[3],[0],[3],[2],[1],[4],[0],[2],[1],[1],[0],[1],[0],[4],[1],[3],[0],[2],[3],[0],[4],[1],[0],[3],[1],[0],[2],[0],[0],[4],[4],[1],[0],[3],[0],[3],[0],[0],[4],[4],[3],[4],[3],[1],[1],[3],[3],[0],[3],[4],[4],[2],[0],[1],[3],[2],[4],[1],[3],[1],[0],[0],[2],[0],[1],[1],[1],[3],[4],[0],[2],[4],[4],[3],[3],[3],[3],[4],[1],[1],[3],[2],[0],[2],[1],[0],[2],[2],[1],[4],[1],[2],[2],[3],[2],[0],[1],[1],[0],[4],[1],[0],[1],[3],[0],[3],[3],[3],[4],[1],[1],[0],[4],[4],[0],[1],[2],[4],[2],[0],[2],[3],[3],[4],[4],[1],[4],[1],[4],[2],[0],[2],[2],[2],[1],[2],[3],[3],[0],[0],[3],[3],[3],[2],[0],[1],[1],[4],[2],[0],[3],[3],[3],[0],[4],[1],[3],[4],[4],[0],[3],[3],[3],[1],[2],[0],[1],[2],[4],[0],[0],[2],[3],[1],[4],[2],[2],[1],[2],[0],[2],[2],[4],[1],[2],[3],[1],[3],[3],[1],[1],[2],[3],[4],[2],[3],[1],[2],[0],[4],[2],[3],[1],[2],[2],[1],[0],[4],[3],[1],[3],[3],[4],[3],[1],[0],[4],[3],[4],[2],[1],[1],[3],[0],[4],[3],[1],[0],[3],[3],[1],[1],[3],[1],[4],[2],[0],[1],[2],[4],[2],[3],[2],[0],[4],[1],[2],[1],[1],[2],[1],[0],[4],[3],[0],[3],[1],[4],[4],[2],[1],[4],[1],[1],[3],[4],[4],[4],[2],[1],[0],[0],[0],[4],[3],[2],[4],[2],[3],[2],[3],[2],[1],[1],[4],[3],[4],[2],[2],[0],[1],[4],[4],[0],[3],[2],[2],[1],[2],[2],[0],[0],[1],[4],[1],[2],[0],[0],[0],[4],[4],[0],[4],[1],[1],[3],[0],[1],[3],[0],[4],[0],[4],[1],[1],[1],[3],[0],[0],[2],[4],[0],[1],[0],[4],[4],[4],[3],[0],[3],[0],[0],[0],[1],[3],[1],[2],[1],[3],[4],[0],[0],[3],[4],[1],[4],[3],[1],[1],[3],[0],[1],[3],[0],[0],[1],[4],[0],[4],[2],[3],[3],[4],[3],[4],[0],[4],[0],[1],[1],[2]],[[3],[1],[0],[3],[4],[0],[2],[4],[1],[4],[3],[3],[1],[2],[4],[2],[2],[1],[3],[1],[1],[4],[3],[3],[0],[4],[1],[2],[1],[0],[3],[2],[1],[2],[0],[4],[2],[1],[4],[4],[0],[0],[1],[2],[2],[1],[3],[0],[3],[1],[2],[2],[1],[1],[3],[1],[1],[0],[3],[4],[4],[2],[4],[0],[4],[1],[2],[4],[3],[1],[2],[0],[3],[0],[0],[1],[2],[1],[3],[3],[1],[4],[4],[0],[0],[2],[1],[4],[0],[2],[0],[0],[2],[2],[3],[0],[0],[2],[4],[3],[1],[2],[1],[2],[1],[4],[0],[0],[0],[2],[1],[3],[4],[0],[0],[4],[3],[3],[0],[1],[3],[3],[3],[3],[4],[3],[3],[0],[0],[0],[1],[2],[0],[1],[1],[0],[2],[3],[4],[3],[2],[4],[4],[3],[2],[3],[1],[1],[4],[4],[2],[0],[3],[0],[2],[1],[1],[3],[2],[0],[4],[0],[3],[0],[1],[0],[0],[0],[1],[0],[4],[0],[4],[4],[0],[2],[1],[0],[1],[1],[1],[1],[0],[0],[2],[4],[0],[4],[2],[0],[0],[4],[3],[4],[1],[4],[3],[0],[3],[2],[4],[4],[2],[1],[3],[0],[3],[0],[0],[2],[0],[0],[1],[3],[4],[2],[3],[4],[0],[1],[4],[2],[3],[2],[0],[3],[1],[1],[1],[4],[2],[4],[4],[1],[0],[1],[2],[0],[1],[4],[4],[2],[0],[3],[2],[0],[2],[1],[1],[4],[1],[3],[0],[3],[3],[4],[1],[1],[2],[2],[4],[4],[4],[0],[1],[4],[2],[1],[1],[4],[1],[3],[3],[2],[0],[0],[3],[4],[3],[4],[4],[4],[3],[1],[1],[4],[3],[0],[4],[0],[4],[3],[1],[2],[3],[0],[2],[1],[0],[2],[1],[3],[1],[3],[3],[0],[3],[4],[2],[0],[3],[4],[0],[0],[0],[3],[4],[4],[2],[2],[4],[4],[4],[4],[2],[4],[1],[3],[4],[0],[4],[1],[4],[4],[4],[2],[3],[4],[1],[3],[4],[1],[3],[4],[3],[1],[4],[2],[0],[4],[1],[0],[4],[3],[1],[4],[1],[2],[0],[1],[3],[0],[2],[1],[3],[2],[4],[2],[4],[0],[1],[0],[0],[0],[3],[0],[2],[1],[4],[1],[0],[0],[4],[3],[4],[3],[4],[0],[2],[3],[1],[1],[3],[1],[2],[4],[4],[4],[2],[0],[1],[0],[0],[4],[0],[0],[2],[0],[1],[2],[0],[4],[4],[2],[3],[0],[2],[0],[2],[2],[2],[1],[1],[3],[3],[2],[0],[4],[2],[4],[3],[1],[2],[4],[2],[4],[2],[4],[1],[3],[3],[3],[4],[4],[1],[2],[3],[0],[1],[0],[0],[4],[4],[1],[4],[1],[4],[0],[4],[4],[3],[1],[2],[1],[3],[4],[4],[3],[1],[4],[3],[2],[1],[2],[4],[4],[0],[2],[0],[2],[0],[2],[4],[3],[3],[1],[1],[0],[4],[3],[3],[0],[4],[4],[2],[2],[4],[3],[1],[4],[3],[1],[3],[1],[0],[4],[4],[0],[3],[3],[4],[4]]]
def setup_inputs(rng):
    return {"x": rng.standard_normal((N, 128, TOK), dtype=np.float32).astype(ml_dtypes.bfloat16), "gate": (0.5 * rng.integers(1, 4, size=(N, K, TOK)) * (2 * rng.integers(0, 2, size=(N, K, TOK)) - 1)).astype(np.float32).astype(ml_dtypes.bfloat16), "w1": (rng.standard_normal((N, 128, FT * 128), dtype=np.float32) / 8).astype(ml_dtypes.bfloat16), "w2": (rng.standard_normal((N, 128, FT * 128), dtype=np.float32) / 8).astype(ml_dtypes.bfloat16)}
def setup_inputs_big(rng):
    d = setup_inputs(rng)
    for k in ("x", "gate", "w1", "w2"): d[k] = (d[k].astype(np.float32) * 1024.0).astype(d[k].dtype)
    return d
def setup_inputs_small(rng):
    d = setup_inputs(rng)
    for k in ("x", "gate", "w1", "w2"): d[k] = (d[k].astype(np.float32) * (1 / 1024.0)).astype(d[k].dtype)
    return d
def reference(x, gate, w1, w2):
    X, GATE, W1, W2 = x.astype(np.float64), gate.astype(np.float64), w1.astype(np.float64), w2.astype(np.float64)
    y = np.zeros((N, 128, TOK))
    for r in range(N):
        for t in range(TOK):
            for i, e in enumerate(ROUTE[r][t]):
                hid = np.maximum(W1[e].T @ X[r][:, t], 0.0)
                y[r][:, t] += GATE[r][i, t] * sum(W2[e][:, 128 * f:128 * f + 128].T @ hid[128 * f:128 * f + 128] for f in range(FT))
    return {"y": y.astype(ml_dtypes.bfloat16)}

@@ -1,0 +1,267 @@
+from concourse.bass import DstId, RemoteDMATransfer
+from concourse.mybir import AluOpType
+
+NSIM = 512
+NE = 5
+TOKS = 512
+HALF = 256
+HELPERS = 16
+BIG = 2.0 ** 80
+
+SCRATCH = {
+    "W": ("sbuf", [128, NE * 256], "bfloat16"),
+    "X": ("sbuf", [128, TOKS], "bfloat16"),
+    "G": ("sbuf", [128, TOKS], "bfloat16"),
+    "ONE": ("sbuf", [128, 128], "bfloat16"),
+    "GB": ("sbuf", [128, TOKS], "float32"),
+    "Z": ("sbuf", [128, HALF], "float32"),
+    "R": ("sbuf", [128, TOKS], "bfloat16"),
+    "C": ("sbuf", [128, NE * 128], "bfloat16"),
+    "H": ("sbuf", [128, NE * TOKS], "bfloat16"),
+    "YS": ("sbuf", [128, TOKS], "bfloat16"),
+    "HP0": ("psum", [128, 512], "float32"),
+    "HP1": ("psum", [128, 512], "float32"),
+    "HP2": ("psum", [128, 512], "float32"),
+    "HP3": ("psum", [128, 512], "float32"),
+    "HP4": ("psum", [128, 512], "float32"),
+    "YP0": ("psum", [128, 512], "float32"),
+    "YP1": ("psum", [128, 512], "float32"),
+    "GP": ("psum", [128, 512], "float32"),
+}
+SEMAPHORES = (["ldw", "ldx", "sent", "msk", "hm", "one", "cl", "zz", "gp", "gb", "st", "yp0", "yp1", "ys0", "ys1"]
+              + ["arr%d" % e for e in range(NE)] + ["hp%d" % e for e in range(NE)]
+              + ["hs%d_%d" % (e, h) for e in range(NE) for h in range(2)])
+
+
+def _bits(mask):
+    return [b for b in range(16) if (mask >> b) & 1]
+
+
+def _tomask(bits):
+    m = 0
+    for b in bits:
+        m |= 1 << b
+    return m
+
+
+def _plan(T, topo):
+    cores = list(T.cores)
+    n = len(cores)
+
+    def key(c):
+        return (topo.host(c), topo.chip(c))
+
+    groups = {}
+    for r in range(n):
+        groups.setdefault(key(cores[r]), []).append(r)
+    hop1 = {r: [] for r in range(n)}
+    hop2 = {r: [] for r in range(n)}
+    turn = {k: 0 for k in groups}
+    for s in range(n):
+        for k, mem in groups.items():
+            if s in mem:
+                hop1[s] += [d for d in mem if d != s]
+            elif topo.may_write(cores[s], cores[mem[0]]):
+                pick = mem[turn[k] % len(mem)]
+                turn[k] += 1
+                hop1[s].append(pick)
+                hop2[pick] += [(s, d) for d in mem if d != pick]
+    for s in range(n):
+        for k, mem in groups.items():
+            if s in mem or topo.may_write(cores[s], cores[mem[0]]):
+                continue
+            for d in mem:
+                cands = [m for m in hop1[s] if topo.may_write(cores[m], cores[d])]
+                m = min(cands, key=lambda q: len(hop2[q]))
+                hop2[m].append((s, d))
+
+    used = set(cores)
+    helpers = {r: [] for r in range(n)}
+    for k, mem in groups.items():
+        free = [c for c in range(NSIM) if key(c) == k and c not in used]
+        for i, c in enumerate(free):
+            helpers[mem[i % len(mem)]].append(c)
+            used.add(c)
+    for r in range(n):
+        cr = cores[r]
+        cand = [c for c in range(NSIM) if c not in used and topo.host(c) == topo.host(cr)
+                and topo.same_plane(c, cr) and topo.may_write(c, cr)]
+        cand.sort(key=lambda c: (topo.die(c) == topo.die(cr), c))
+        helpers[r] = helpers[r][:HELPERS]
+        for c in cand[:HELPERS - len(helpers[r])]:
+            helpers[r].append(c)
+            used.add(c)
+    job = {}
+    for r in range(n):
+        for i, c in enumerate(helpers[r]):
+            job[c] = (r, i)
+
+    calls = {r: [] for r in range(n)}
+    cnt = {}
+    stage = {}
+    for r in range(n):
+        c = cores[r]
+        offbits = []
+        for lst in ([(r, d) for d in hop1[r]], hop2[r]):
+            for (_, d) in lst:
+                if key(cores[d]) != key(c):
+                    offbits = _bits(topo.mask(c, cores[d]))
+        for hop, lst in ((1, [(r, d) for d in hop1[r]]), (2, hop2[r])):
+            off = [(e, d) for (e, d) in lst if key(cores[d]) != key(c)]
+            on = [(e, d) for (e, d) in lst if key(cores[d]) == key(c)]
+            off.sort(key=lambda ed: not topo.same_plane(c, cores[ed[1]]))
+            for part, isoff in ((off, True), (on, False)):
+                if not part:
+                    continue
+                w = 1
+                while w < len(part):
+                    w *= 2
+                trs = []
+                for i, (e, d) in enumerate(part):
+                    if isoff:
+                        bits = _bits(topo.mask(c, cores[d]))[i::w]
+                    else:
+                        rest = [b for b in _bits(topo.mask(c, cores[d])) if b not in offbits]
+                        bits = rest[i::w][:4]
+                    trs.append((e, d, _tomask(bits)))
+                    cnt[(e, d)] = len(bits)
+                    stage[(e, d)] = (hop, isoff)
+                calls[r].append((sorted(set(e for (e, _) in part if e != r)), trs))
+    return calls, cnt, stage, helpers, job
+
+
+def _paint(g, core, T, topo, r, i):
+    route = T.tables["ROUTE"][r]
+    w = TOKS // HELPERS
+    c0 = i * w
+    S = T.sem
+    v = g.vector
+    v.memset(T.R[:, c0:c0 + w], 1.0).then_inc(S.hm, 1)
+    v.wait_ge(S.hm, 1)
+    n = 1
+    a = c0
+    while a < c0 + w:
+        b = a + 1
+        while b < c0 + w and route[b][0] == route[a][0]:
+            b += 1
+        v.memset(T.R[0:route[a][0] + 1, a:b], -1.0).then_inc(S.hm, 1)
+        n += 1
+        a = b
+    dst = T.cores[r]
+    bits = _bits(topo.mask(core, dst))[:8]
+    rid, pid = topo.addr(dst, core)
+    g.wait_ge(S.hm, n)
+    g.remote_dma(out_ap=T.R[:, c0:c0 + w], in_ap=T.R[:, c0:c0 + w], remote_sem=S.msk, local_sem=S.sent,
+                 pid=pid, routing_id=rid, dma_engine_mask=_tomask(bits))
+    g.wait_ge(S.sent, len(bits))
+
+
+def rank_program(g, core, T, topo):
+    calls, cnt, stage, helpers, job = _plan(T, topo)
+    rank = T.rank_of(core)
+    if rank is None:
+        if core in job:
+            _paint(g, core, T, topo, job[core][0], job[core][1])
+        return
+    S = T.sem
+    cores = list(T.cores)
+    pe, v = g.tensor, g.vector
+
+    def w1(e):
+        return T.W[:, e * 256:e * 256 + 128]
+
+    def w2(e):
+        return T.W[:, e * 256 + 128:e * 256 + 256]
+
+    def slot(e):
+        return T.W[:, e * 256:e * 256 + 256]
+
+    g.sync.dma_start(w1(rank), T.w1[:, :]).then_inc(S.ldw, 16)
+    g.scalar.dma_start(w2(rank), T.w2[:, :]).then_inc(S.ldw, 16)
+    g.sync.dma_start(T.X[:, :], T.x[:, :]).then_inc(S.ldx, 16)
+    g.scalar.dma_start(T.G[0:1, :], T.gate[:, :]).then_inc(S.ldx, 16)
+
+    g.wait_ge(S.ldw, 32)
+    sent = 0
+    for waits, trs in calls[rank]:
+        for e in waits:
+            g.wait_ge(S["arr%d" % e], cnt[(e, rank)])
+        lst = []
+        for (e, d, m) in trs:
+            rid, pid = topo.addr(cores[d], core)
+            lst.append(RemoteDMATransfer(dst_ids=[DstId(rid=rid, pnc=pid)], dma_engine_mask=m,
+                                         remote_sem=S["arr%d" % e], src=slot(e), dst=slot(e)))
+            sent += len(_bits(m))
+        g.remote_dma_fused(lst, local_sem=S.sent)
+
+    v.memset(T.ONE[0:1, :], 1.0).then_inc(S.one, 1)
+    v.memset(T.C[0:NE, :], BIG / 2).then_inc(S.cl, 1)
+    v.wait_ge(S.cl, 1)
+    for e in range(1, NE):
+        v.memset(T.C[0:e + 1, e * 128:(e + 1) * 128], -BIG / 2).then_inc(S.cl, 1)
+    v.wait_ge(S.cl, NE)
+    v.memset(T.C[0:1, :], 2 * BIG).then_inc(S.cl, 1)
+    v.memset(T.Z[:, :], 0.0).then_inc(S.zz, 1)
+
+    others = sorted([e for e in range(NE) if e != rank], key=lambda e: (stage[(e, rank)], e))
+    early = [e for e in others if stage[(e, rank)][0] == 1]
+    late = [e for e in others if stage[(e, rank)][0] == 2]
+    order = [rank] + early + late
+    nmask = sum(len(_bits(topo.mask(c, core))[:8]) for c in helpers[rank])
+
+    def mm_mask(e):
+        pe.matmul(T["HP%d" % e][:, :], T.C[0:NE, e * 128:(e + 1) * 128], T.R[0:NE, :], True, False).then_inc(S["hp%d" % e], 1)
+
+    def mm_w1(e):
+        pe.matmul(T["HP%d" % e][:, :], w1(e), T.X[:, :], False, True).then_inc(S["hp%d" % e], 1)
+
+    def mm_w2(e):
+        for h in range(2):
+            pe.wait_ge(S["hs%d_%d" % (e, h)], 1)
+            pe.matmul(T["YP%d" % h][:, 0:HALF], w2(e), T.H[:, e * TOKS + h * HALF:e * TOKS + (h + 1) * HALF],
+                      e == order[0], e == order[-1]).then_inc(S["yp%d" % h], 1)
+
+    pe.wait_ge(S.one, 1)
+    pe.wait_ge(S.ldx, 32)
+    pe.matmul(T.GP[:, :], T.ONE[0:1, :], T.G[0:1, :], True, True).then_inc(S.gp, 1)
+    pe.wait_ge(S.cl, NE + 1)
+    pe.wait_ge(S.msk, nmask)
+    mm_mask(rank)
+    pe.wait_ge(S.ldw, 32)
+    mm_w1(rank)
+    for e in early:
+        mm_mask(e)
+    for e in early:
+        pe.wait_ge(S["arr%d" % e], cnt[(e, rank)])
+        mm_w1(e)
+    for e in late:
+        mm_mask(e)
+    mm_w2(rank)
+    for e in early:
+        mm_w2(e)
+    for e in late:
+        pe.wait_ge(S["arr%d" % e], cnt[(e, rank)])
+        mm_w1(e)
+    for e in late:
+        mm_w2(e)
+
+    v.wait_ge(S.gp, 1)
+    v.tensor_copy(T.GB[:, :], T.GP[:, :]).then_inc(S.gb, 1)
+    v.wait_ge(S.zz, 1)
+    for e in order:
+        v.wait_ge(S["hp%d" % e], 2)
+        for h in range(2):
+            v.tensor_tensor(T.H[:, e * TOKS + h * HALF:e * TOKS + (h + 1) * HALF],
+                            T["HP%d" % e][:, h * HALF:(h + 1) * HALF], T.Z[:, :], AluOpType.max).then_inc(S["hs%d_%d" % (e, h)], 1)
+    v.wait_ge(S.gb, 1)
+    for h in range(2):
+        v.wait_ge(S["yp%d" % h], NE)
+        v.tensor_tensor(T.YS[:, h * HALF:(h + 1) * HALF], T["YP%d" % h][:, 0:HALF],
+                        T.GB[:, h * HALF:(h + 1) * HALF], AluOpType.mult).then_inc(S["ys%d" % h], 1)
+
+    g.sync.wait_ge(S.ys0, 1)
+    g.sync.dma_start(T.y[:, 0:HALF], T.YS[:, 0:HALF]).then_inc(S.st, 16)
+    g.scalar.wait_ge(S.ys1, 1)
+    g.scalar.dma_start(T.y[:, HALF:TOKS], T.YS[:, HALF:TOKS]).then_inc(S.st, 16)
+    g.wait_ge(S.sent, sent)
+    g.wait_ge(S.st, 32)

@@ -5,8 +5,9 @@ NSIM = 512
 NE = 5
 TOKS = 512
 HALF = 256
-HELPERS = 16
+HELPERS = 32
 BIG = 2.0 ** 80
+WHOLE = 2
 
 SCRATCH = {
     "W": ("sbuf", [128, NE * 256], "bfloat16"),
@@ -29,7 +30,7 @@ SCRATCH = {
     "GP": ("psum", [128, 512], "float32"),
 }
 SEMAPHORES = (["ldw", "ldx", "sent", "msk", "hm", "one", "cl", "zz", "gp", "gb", "st", "yp0", "yp1", "ys0", "ys1"]
-              + ["arr%d" % e for e in range(NE)] + ["hp%d" % e for e in range(NE)]
+              + ["a%d_%d" % (e, p) for e in range(NE) for p in range(2)] + ["hp%d" % e for e in range(NE)]
               + ["hs%d_%d" % (e, h) for e in range(NE) for h in range(2)])
 
 
@@ -84,9 +85,8 @@ def _plan(T, topo):
             used.add(c)
     for r in range(n):
         cr = cores[r]
-        cand = [c for c in range(NSIM) if c not in used and topo.host(c) == topo.host(cr)
-                and topo.same_plane(c, cr) and topo.may_write(c, cr)]
-        cand.sort(key=lambda c: (topo.die(c) == topo.die(cr), c))
+        cand = [c for c in range(NSIM) if c not in used and topo.same_plane(c, cr) and topo.may_write(c, cr)]
+        cand.sort(key=lambda c: (topo.host(c) != topo.host(cr), topo.die(c) == topo.die(cr), c))
         helpers[r] = helpers[r][:HELPERS]
         for c in cand[:HELPERS - len(helpers[r])]:
             helpers[r].append(c)
@@ -116,6 +116,7 @@ def _plan(T, topo):
                 w = 1
                 while w < len(part):
                     w *= 2
+                whole = hop == 1 and not isoff
                 trs = []
                 for i, (e, d) in enumerate(part):
                     if isoff:
@@ -124,9 +125,11 @@ def _plan(T, topo):
                         rest = [b for b in _bits(topo.mask(c, cores[d])) if b not in offbits]
                         bits = rest[i::w][:4]
                     trs.append((e, d, _tomask(bits)))
-                    cnt[(e, d)] = len(bits)
+                    cnt[(e, d)] = (len(bits), whole)
                     stage[(e, d)] = (hop, isoff)
-                calls[r].append((sorted(set(e for (e, _) in part if e != r)), trs))
+                waits = sorted(set(e for (e, _) in part if e != r))
+                for piece in ([WHOLE] if whole else [0, 1]):
+                    calls[r].append((piece, waits, trs))
     return calls, cnt, stage, helpers, job
 
 
@@ -173,8 +176,12 @@ def rank_program(g, core, T, topo):
     def w2(e):
         return T.W[:, e * 256 + 128:e * 256 + 256]
 
-    def slot(e):
-        return T.W[:, e * 256:e * 256 + 256]
+    def part(e, piece):
+        return (w1(e), w2(e), T.W[:, e * 256:e * 256 + 256])[piece]
+
+    def wait_piece(q, e, piece):
+        k, whole = cnt[(e, rank)]
+        q.wait_ge(S["a%d_%d" % (e, 0 if whole else piece)], k)
 
     g.sync.dma_start(w1(rank), T.w1[:, :]).then_inc(S.ldw, 16)
     g.scalar.dma_start(w2(rank), T.w2[:, :]).then_inc(S.ldw, 16)
@@ -183,14 +190,14 @@ def rank_program(g, core, T, topo):
 
     g.wait_ge(S.ldw, 32)
     sent = 0
-    for waits, trs in calls[rank]:
+    for piece, waits, trs in calls[rank]:
         for e in waits:
-            g.wait_ge(S["arr%d" % e], cnt[(e, rank)])
+            wait_piece(g, e, piece)
         lst = []
         for (e, d, m) in trs:
             rid, pid = topo.addr(cores[d], core)
             lst.append(RemoteDMATransfer(dst_ids=[DstId(rid=rid, pnc=pid)], dma_engine_mask=m,
-                                         remote_sem=S["arr%d" % e], src=slot(e), dst=slot(e)))
+                                         remote_sem=S["a%d_%d" % (e, piece % 2)], src=part(e, piece), dst=part(e, piece)))
             sent += len(_bits(m))
         g.remote_dma_fused(lst, local_sem=S.sent)
 
@@ -209,13 +216,17 @@ def rank_program(g, core, T, topo):
     order = [rank] + early + late
     nmask = sum(len(_bits(topo.mask(c, core))[:8]) for c in helpers[rank])
 
-    def mm_mask(e):
-        pe.matmul(T["HP%d" % e][:, :], T.C[0:NE, e * 128:(e + 1) * 128], T.R[0:NE, :], True, False).then_inc(S["hp%d" % e], 1)
+    def mm_mask(e, first):
+        pe.matmul(T["HP%d" % e][:, :], T.C[0:NE, e * 128:(e + 1) * 128], T.R[0:NE, :], first, not first).then_inc(S["hp%d" % e], 1)
 
-    def mm_w1(e):
-        pe.matmul(T["HP%d" % e][:, :], w1(e), T.X[:, :], False, True).then_inc(S["hp%d" % e], 1)
+    def mm_w1(e, first):
+        if e != rank:
+            wait_piece(pe, e, 0)
+        pe.matmul(T["HP%d" % e][:, :], w1(e), T.X[:, :], first, not first).then_inc(S["hp%d" % e], 1)
 
     def mm_w2(e):
+        if e != rank:
+            wait_piece(pe, e, 1)
         for h in range(2):
             pe.wait_ge(S["hs%d_%d" % (e, h)], 1)
             pe.matmul(T["YP%d" % h][:, 0:HALF], w2(e), T.H[:, e * TOKS + h * HALF:e * TOKS + (h + 1) * HALF],
@@ -224,24 +235,20 @@ def rank_program(g, core, T, topo):
     pe.wait_ge(S.one, 1)
     pe.wait_ge(S.ldx, 32)
     pe.matmul(T.GP[:, :], T.ONE[0:1, :], T.G[0:1, :], True, True).then_inc(S.gp, 1)
+    pe.wait_ge(S.ldw, 32)
+    mm_w1(rank, True)
     pe.wait_ge(S.cl, NE + 1)
     pe.wait_ge(S.msk, nmask)
-    mm_mask(rank)
-    pe.wait_ge(S.ldw, 32)
-    mm_w1(rank)
-    for e in early:
-        mm_mask(e)
-    for e in early:
-        pe.wait_ge(S["arr%d" % e], cnt[(e, rank)])
-        mm_w1(e)
-    for e in late:
-        mm_mask(e)
+    mm_mask(rank, False)
+    for e in early + late:
+        mm_mask(e, True)
     mm_w2(rank)
+    for e in early:
+        mm_w1(e, False)
     for e in early:
         mm_w2(e)
     for e in late:
-        pe.wait_ge(S["arr%d" % e], cnt[(e, rank)])
-        mm_w1(e)
+        mm_w1(e, False)
     for e in late:
         mm_w2(e)
 

from concourse.bass import DstId, RemoteDMATransfer
from concourse.mybir import AluOpType

NSIM = 512
NE = 5
TOKS = 512
HALF = 256
HELPERS = 32
BIG = 2.0 ** 80
WHOLE = 2

SCRATCH = {
    "W": ("sbuf", [128, NE * 256], "bfloat16"),
    "X": ("sbuf", [128, TOKS], "bfloat16"),
    "G": ("sbuf", [128, TOKS], "bfloat16"),
    "ONE": ("sbuf", [128, 128], "bfloat16"),
    "GB": ("sbuf", [128, TOKS], "float32"),
    "Z": ("sbuf", [128, HALF], "float32"),
    "R": ("sbuf", [128, TOKS], "bfloat16"),
    "C": ("sbuf", [128, NE * 128], "bfloat16"),
    "H": ("sbuf", [128, NE * TOKS], "bfloat16"),
    "YS": ("sbuf", [128, TOKS], "bfloat16"),
    "HP0": ("psum", [128, 512], "float32"),
    "HP1": ("psum", [128, 512], "float32"),
    "HP2": ("psum", [128, 512], "float32"),
    "HP3": ("psum", [128, 512], "float32"),
    "HP4": ("psum", [128, 512], "float32"),
    "YP0": ("psum", [128, 512], "float32"),
    "YP1": ("psum", [128, 512], "float32"),
    "GP": ("psum", [128, 512], "float32"),
}
SEMAPHORES = (["ldw", "ldx", "sent", "msk", "hm", "one", "cl", "zz", "gp", "gb", "st", "yp0", "yp1", "ys0", "ys1"]
              + ["a%d_%d" % (e, p) for e in range(NE) for p in range(2)] + ["hp%d" % e for e in range(NE)]
              + ["hs%d_%d" % (e, h) for e in range(NE) for h in range(2)])


def _bits(mask):
    return [b for b in range(16) if (mask >> b) & 1]


def _tomask(bits):
    m = 0
    for b in bits:
        m |= 1 << b
    return m


def _plan(T, topo):
    cores = list(T.cores)
    n = len(cores)

    def key(c):
        return (topo.host(c), topo.chip(c))

    groups = {}
    for r in range(n):
        groups.setdefault(key(cores[r]), []).append(r)
    hop1 = {r: [] for r in range(n)}
    hop2 = {r: [] for r in range(n)}
    turn = {k: 0 for k in groups}
    for s in range(n):
        for k, mem in groups.items():
            if s in mem:
                hop1[s] += [d for d in mem if d != s]
            elif topo.may_write(cores[s], cores[mem[0]]):
                pick = mem[turn[k] % len(mem)]
                turn[k] += 1
                hop1[s].append(pick)
                hop2[pick] += [(s, d) for d in mem if d != pick]
    for s in range(n):
        for k, mem in groups.items():
            if s in mem or topo.may_write(cores[s], cores[mem[0]]):
                continue
            for d in mem:
                cands = [m for m in hop1[s] if topo.may_write(cores[m], cores[d])]
                m = min(cands, key=lambda q: len(hop2[q]))
                hop2[m].append((s, d))

    used = set(cores)
    helpers = {r: [] for r in range(n)}
    for k, mem in groups.items():
        free = [c for c in range(NSIM) if key(c) == k and c not in used]
        for i, c in enumerate(free):
            helpers[mem[i % len(mem)]].append(c)
            used.add(c)
    for r in range(n):
        cr = cores[r]
        cand = [c for c in range(NSIM) if c not in used and topo.same_plane(c, cr) and topo.may_write(c, cr)]
        cand.sort(key=lambda c: (topo.host(c) != topo.host(cr), topo.die(c) == topo.die(cr), c))
        helpers[r] = helpers[r][:HELPERS]
        for c in cand[:HELPERS - len(helpers[r])]:
            helpers[r].append(c)
            used.add(c)
    job = {}
    for r in range(n):
        for i, c in enumerate(helpers[r]):
            job[c] = (r, i)

    calls = {r: [] for r in range(n)}
    cnt = {}
    stage = {}
    for r in range(n):
        c = cores[r]
        offbits = []
        for lst in ([(r, d) for d in hop1[r]], hop2[r]):
            for (_, d) in lst:
                if key(cores[d]) != key(c):
                    offbits = _bits(topo.mask(c, cores[d]))
        for hop, lst in ((1, [(r, d) for d in hop1[r]]), (2, hop2[r])):
            off = [(e, d) for (e, d) in lst if key(cores[d]) != key(c)]
            on = [(e, d) for (e, d) in lst if key(cores[d]) == key(c)]
            off.sort(key=lambda ed: not topo.same_plane(c, cores[ed[1]]))
            for part, isoff in ((off, True), (on, False)):
                if not part:
                    continue
                w = 1
                while w < len(part):
                    w *= 2
                whole = hop == 1 and not isoff
                trs = []
                for i, (e, d) in enumerate(part):
                    if isoff:
                        bits = _bits(topo.mask(c, cores[d]))[i::w]
                    else:
                        rest = [b for b in _bits(topo.mask(c, cores[d])) if b not in offbits]
                        bits = rest[i::w][:4]
                    trs.append((e, d, _tomask(bits)))
                    cnt[(e, d)] = (len(bits), whole)
                    stage[(e, d)] = (hop, isoff)
                waits = sorted(set(e for (e, _) in part if e != r))
                for piece in ([WHOLE] if whole else [0, 1]):
                    calls[r].append((piece, waits, trs))
    return calls, cnt, stage, helpers, job


def _paint(g, core, T, topo, r, i):
    route = T.tables["ROUTE"][r]
    w = TOKS // HELPERS
    c0 = i * w
    S = T.sem
    v = g.vector
    v.memset(T.R[:, c0:c0 + w], 1.0).then_inc(S.hm, 1)
    v.wait_ge(S.hm, 1)
    n = 1
    a = c0
    while a < c0 + w:
        b = a + 1
        while b < c0 + w and route[b][0] == route[a][0]:
            b += 1
        v.memset(T.R[0:route[a][0] + 1, a:b], -1.0).then_inc(S.hm, 1)
        n += 1
        a = b
    dst = T.cores[r]
    bits = _bits(topo.mask(core, dst))[:8]
    rid, pid = topo.addr(dst, core)
    g.wait_ge(S.hm, n)
    g.remote_dma(out_ap=T.R[:, c0:c0 + w], in_ap=T.R[:, c0:c0 + w], remote_sem=S.msk, local_sem=S.sent,
                 pid=pid, routing_id=rid, dma_engine_mask=_tomask(bits))
    g.wait_ge(S.sent, len(bits))


def rank_program(g, core, T, topo):
    calls, cnt, stage, helpers, job = _plan(T, topo)
    rank = T.rank_of(core)
    if rank is None:
        if core in job:
            _paint(g, core, T, topo, job[core][0], job[core][1])
        return
    S = T.sem
    cores = list(T.cores)
    pe, v = g.tensor, g.vector

    def w1(e):
        return T.W[:, e * 256:e * 256 + 128]

    def w2(e):
        return T.W[:, e * 256 + 128:e * 256 + 256]

    def part(e, piece):
        return (w1(e), w2(e), T.W[:, e * 256:e * 256 + 256])[piece]

    def wait_piece(q, e, piece):
        k, whole = cnt[(e, rank)]
        q.wait_ge(S["a%d_%d" % (e, 0 if whole else piece)], k)

    g.sync.dma_start(w1(rank), T.w1[:, :]).then_inc(S.ldw, 16)
    g.scalar.dma_start(w2(rank), T.w2[:, :]).then_inc(S.ldw, 16)
    g.sync.dma_start(T.X[:, :], T.x[:, :]).then_inc(S.ldx, 16)
    g.scalar.dma_start(T.G[0:1, :], T.gate[:, :]).then_inc(S.ldx, 16)

    g.wait_ge(S.ldw, 32)
    sent = 0
    for piece, waits, trs in calls[rank]:
        for e in waits:
            wait_piece(g, e, piece)
        lst = []
        for (e, d, m) in trs:
            rid, pid = topo.addr(cores[d], core)
            lst.append(RemoteDMATransfer(dst_ids=[DstId(rid=rid, pnc=pid)], dma_engine_mask=m,
                                         remote_sem=S["a%d_%d" % (e, piece % 2)], src=part(e, piece), dst=part(e, piece)))
            sent += len(_bits(m))
        g.remote_dma_fused(lst, local_sem=S.sent)

    v.memset(T.ONE[0:1, :], 1.0).then_inc(S.one, 1)
    v.memset(T.C[0:NE, :], BIG / 2).then_inc(S.cl, 1)
    v.wait_ge(S.cl, 1)
    for e in range(1, NE):
        v.memset(T.C[0:e + 1, e * 128:(e + 1) * 128], -BIG / 2).then_inc(S.cl, 1)
    v.wait_ge(S.cl, NE)
    v.memset(T.C[0:1, :], 2 * BIG).then_inc(S.cl, 1)
    v.memset(T.Z[:, :], 0.0).then_inc(S.zz, 1)

    others = sorted([e for e in range(NE) if e != rank], key=lambda e: (stage[(e, rank)], e))
    early = [e for e in others if stage[(e, rank)][0] == 1]
    late = [e for e in others if stage[(e, rank)][0] == 2]
    order = [rank] + early + late
    nmask = sum(len(_bits(topo.mask(c, core))[:8]) for c in helpers[rank])

    def mm_mask(e, first):
        pe.matmul(T["HP%d" % e][:, :], T.C[0:NE, e * 128:(e + 1) * 128], T.R[0:NE, :], first, not first).then_inc(S["hp%d" % e], 1)

    def mm_w1(e, first):
        if e != rank:
            wait_piece(pe, e, 0)
        pe.matmul(T["HP%d" % e][:, :], w1(e), T.X[:, :], first, not first).then_inc(S["hp%d" % e], 1)

    def mm_w2(e):
        if e != rank:
            wait_piece(pe, e, 1)
        for h in range(2):
            pe.wait_ge(S["hs%d_%d" % (e, h)], 1)
            pe.matmul(T["YP%d" % h][:, 0:HALF], w2(e), T.H[:, e * TOKS + h * HALF:e * TOKS + (h + 1) * HALF],
                      e == order[0], e == order[-1]).then_inc(S["yp%d" % h], 1)

    pe.wait_ge(S.one, 1)
    pe.wait_ge(S.ldx, 32)
    pe.matmul(T.GP[:, :], T.ONE[0:1, :], T.G[0:1, :], True, True).then_inc(S.gp, 1)
    pe.wait_ge(S.ldw, 32)
    mm_w1(rank, True)
    pe.wait_ge(S.cl, NE + 1)
    pe.wait_ge(S.msk, nmask)
    mm_mask(rank, False)
    for e in early + late:
        mm_mask(e, True)
    mm_w2(rank)
    for e in early:
        mm_w1(e, False)
    for e in early:
        mm_w2(e)
    for e in late:
        mm_w1(e, False)
    for e in late:
        mm_w2(e)

    v.wait_ge(S.gp, 1)
    v.tensor_copy(T.GB[:, :], T.GP[:, :]).then_inc(S.gb, 1)
    v.wait_ge(S.zz, 1)
    for e in order:
        v.wait_ge(S["hp%d" % e], 2)
        for h in range(2):
            v.tensor_tensor(T.H[:, e * TOKS + h * HALF:e * TOKS + (h + 1) * HALF],
                            T["HP%d" % e][:, h * HALF:(h + 1) * HALF], T.Z[:, :], AluOpType.max).then_inc(S["hs%d_%d" % (e, h)], 1)
    v.wait_ge(S.gb, 1)
    for h in range(2):
        v.wait_ge(S["yp%d" % h], NE)
        v.tensor_tensor(T.YS[:, h * HALF:(h + 1) * HALF], T["YP%d" % h][:, 0:HALF],
                        T.GB[:, h * HALF:(h + 1) * HALF], AluOpType.mult).then_inc(S["ys%d" % h], 1)

    g.sync.wait_ge(S.ys0, 1)
    g.sync.dma_start(T.y[:, 0:HALF], T.YS[:, 0:HALF]).then_inc(S.st, 16)
    g.scalar.wait_ge(S.ys1, 1)
    g.scalar.dma_start(T.y[:, HALF:TOKS], T.YS[:, HALF:TOKS]).then_inc(S.st, 16)
    g.wait_ge(S.sent, sent)
    g.wait_ge(S.st, 32)
